import numpy as np
CORES = [7,6,5,4,3,2,1,0]
N = 8
def setup_inputs(rng):
    return {"x": rng.standard_normal((N, 128, 2048), dtype=np.float32)}
def reference(x):
    s = x.sum(axis=0, dtype=np.float64).astype(x.dtype)
    b = 2048 // N
    return {"y": np.stack([s[:, r * b:(r + 1) * b] for r in range(N)])}

from concourse.bass import DstId, RemoteDMATransfer
from concourse.mybir import AluOpType

B = 256
PIECE_ENGINES = 2
FOLD_ENGINES = 16

SCRATCH = {
    "xs": ("sbuf", [128, 2048], "float32"),
    "gather": ("sbuf", [128, 6 * B], "float32"),
    "others": ("sbuf", [128, B], "float32"),
}
SEMAPHORES = ["loaded", "seeded", "stored", "gathered", "folded", "sent"]


def helper_of(core, cores, topo):
    mates = sorted(c for c in cores if topo.die(c) == topo.die(core))
    return mates[(mates.index(core) + 1) % len(mates)]


def rank_program(g, core, T, topo):
    rank = T.rank_of(core)
    if rank is None:
        return
    cores = list(T.cores)
    helper = {c: helper_of(c, cores, topo) for c in cores}
    helped = {h: o for o, h in helper.items()}

    def block(buf, owner):
        k = T.rank_of(owner)
        return buf[:, k * B:(k + 1) * B]

    def senders(h):
        return [c for c in cores if c != h and c != helped[h]]

    def dst_id(c):
        a = topo.addr(c)
        return DstId(rid=a[0], pnc=a[1])

    g.dma_start(T.xs[:], T.x[:]).then_inc(T.sem.loaded, 16)
    g.dma_start(T.y[:], block(T.x, core)).then_inc(T.sem.seeded, 16)
    g.wait_ge(T.sem.loaded, 16)

    copies = []
    for h in cores:
        if h == core or h == helper[core]:
            continue
        slot = senders(h).index(core)
        copies.append(RemoteDMATransfer(
            dst_ids=[dst_id(h)],
            dma_engine_mask=((1 << PIECE_ENGINES) - 1) << (PIECE_ENGINES * len(copies)),
            remote_sem=T.sem.gathered,
            srcs=[block(T.xs, helped[h])],
            dsts=[T.gather[:, slot * B:(slot + 1) * B]],
            alu_op=0,
        ))
    g.remote_dma_fused(copies, local_sem=T.sem.sent)

    g.wait_ge(T.sem.gathered, 6 * PIECE_ENGINES)
    owner = helped[core]
    g.remote_dma_fused([RemoteDMATransfer(
        dst_ids=[dst_id(owner)],
        dma_engine_mask=(1 << FOLD_ENGINES) - 1,
        remote_sem=T.sem.folded,
        srcs=[block(T.xs, owner)] + [T.gather[:, s * B:(s + 1) * B] for s in range(6)],
        dsts=[T.others[:]],
        alu_op=1,
    )], local_sem=T.sem.sent)

    g.wait_ge(T.sem.seeded, 16)
    g.wait_ge(T.sem.folded, FOLD_ENGINES)
    g.dma_start(T.y[:], T.others[:], accum_op=AluOpType.add).then_inc(T.sem.stored, 16)
    g.wait_ge(T.sem.stored, 16)
    g.wait_ge(T.sem.sent, 6 * PIECE_ENGINES + FOLD_ENGINES)
